import numpy as np
import ml_dtypes


def mxq(x, axis, fmt="e4m3"):
    dtype, down = {"e4m3": (ml_dtypes.float8_e4m3fn, 7), "e5m2": (ml_dtypes.float8_e5m2, 14)}[fmt]
    v = np.moveaxis(np.asarray(x, np.float32).astype(ml_dtypes.bfloat16).astype(np.float64), axis, -1)
    blocks = v.reshape(v.shape[:-1] + (-1, 32))
    amax = np.abs(blocks).max(-1, keepdims=True)
    byte = np.maximum(np.where(amax > 0, np.frexp(amax)[1] - 1 + 127, 0) - down, 1)
    scale = np.exp2(byte - 127.0)
    codes = (blocks / scale).astype(np.float32).astype(dtype).astype(np.float64)
    return np.moveaxis((codes * scale).reshape(v.shape), -1, axis)


WIDE = False


def mx_kscale(k):
    if not WIDE:
        return np.ones(k)
    levels = np.array([10, -10, 5, -5, 0])
    if k % 512:
        return np.exp2(np.random.permutation(np.resize(levels, k // 32))).repeat(32)
    a = np.empty((k // 512, 16))
    for p in range(k // 512):
        a[p, :8] = np.random.permutation(np.resize(levels, 8))
        for g in range(8):
            far = levels[np.abs(levels - a[p, g]) >= 10]
            a[p, g + 8] = far[np.random.randint(len(far))]
    return np.exp2(a.ravel()).repeat(32)


def f64(x):
    return np.asarray(x).astype(np.float64)


def striped(idx):
    return np.tile(idx.reshape(-1, 16).T, (8, 1)).astype(np.uint16)


def unstriped(offs):
    return offs[:16].T.reshape(-1).astype(np.int64)


K, T, D, S, V, N = 1024, 2048, 3, 768, 256, 512
P = 2 ** 7


def setup_inputs():
    n = np.random.standard_normal
    s = mx_kscale(K)[:, None]
    return {
        "xT": (n((K, T)) * s / np.sqrt(D)).astype(ml_dtypes.bfloat16).astype(np.float32),
        "w": (n((K, N)) / np.sqrt(K) / s).astype(np.float32),
        "b": (0.3 * n((N, 1))).astype(np.float32),
        "gate": np.tile(np.random.uniform(0.5, 1.5, (D, 1, V)), (1, P, 1)).astype(ml_dtypes.bfloat16).astype(np.float32),
        "offs": striped(np.concatenate([np.random.permutation(T)[:V] for _ in range(D)])),
    }


def reference(xT, w, b, gate, offs):
    idx = unstriped(offs)
    x = sum(f64(gate)[d, :1] * f64(xT)[:, idx[d * V:(d + 1) * V]] for d in range(D))
    return (mxq(f64(w), 0, "e4m3").T @ mxq(x, 0, "e4m3")) + f64(b)

@@ -1,0 +1,139 @@
+from contextlib import ExitStack
+
+import concourse.mybir as mybir
+from concourse.masks import make_identity
+
+K, T, D, V, N = 1024, 2048, 3, 256, 512
+FLOPS = 2 * K * N * V
+
+F32 = mybir.dt.float32
+BF16 = mybir.dt.bfloat16
+U32 = mybir.dt.uint32
+U16 = mybir.dt.uint16
+U8 = mybir.dt.uint8
+FP8X4 = mybir.dt.float8_e4m3fn_x4
+MULT = mybir.AluOpType.mult
+ADD = mybir.AluOpType.add
+IDENT = mybir.ActivationFunctionType.Identity
+
+P = 128
+PACK = 4
+K_PASS = P * PACK
+PASSES = K // K_PASS
+HALF = 256
+HALVES = N // HALF
+RUN = 4
+COLS = V // 16
+
+
+def tile_picked_bag_lin_bias_sub_l_kernel(tc, xT, w, b, gate, offs, out):
+    nc = tc.nc
+    with ExitStack() as ctx:
+        keep = ctx.enter_context(tc.tile_pool(name="keep", bufs=1))
+        psum = ctx.enter_context(tc.psum_pool(name="psum", bufs=1))
+
+        offsets = keep.tile([P, D * COLS], U16, name="offsets")
+        nc.sync.dma_start(offsets[:], offs)
+        gates = keep.tile([P, D, V], F32, name="gates")
+        nc.sync.dma_start(gates[:], gate.rearrange("d p v -> p d v"))
+
+        x_rows = xT.rearrange("(c p t) n -> c t p n", p=P, t=PACK)
+        w_rows = w.rearrange("(c p j) (h m) -> c h p j m", p=P, j=PACK, m=HALF)
+        planes, w_raw = {}, {}
+        order = [("x", 0, 0), ("x", 0, 1), ("x", 0, 2), ("x", 0, 3), ("x", 1, 0), ("w", 0, 0), ("x", 1, 1),
+                 ("x", 1, 2), ("w", 0, 1), ("x", 1, 3), ("w", 1, 0), ("w", 1, 1)]
+        for kind, c, i in order:
+            if kind == "x":
+                planes[c, i] = keep.tile([P, T], F32, name=f"plane{c}{i}")
+                nc.sync.dma_start(planes[c, i][:], x_rows[c, i])
+            else:
+                w_raw[c, i] = keep.tile([P, PACK, HALF], F32, name=f"wraw{c}{i}")
+                nc.sync.dma_start(w_raw[c, i][:], w_rows[c, i])
+
+        ident = keep.tile([P, P], F32, name="ident")
+        make_identity(nc, ident[:])
+        bias_rows = keep.tile([P, P], F32, name="bias_rows")
+        nc.gpsimd.memset(bias_rows[:], 0.0)
+        nc.scalar.dma_start(bias_rows[0 : N // P, :], b.rearrange("(t p) o -> t (p o)", p=P))
+        bias_ps = psum.tile([P, P], F32, name="bias_ps")
+        nc.tensor.transpose(bias_ps[:], bias_rows[:], ident[:])
+        bias = keep.tile([P, 8], F32, name="bias")
+        nc.scalar.activation(bias[:], bias_ps[:, 0:8], IDENT)
+
+        w_codes, w_scales = {}, {}
+
+        def prepare_w(c, h):
+            wg = keep.tile([P, HALF, PACK], BF16, name=f"wg{c}{h}", align_bytes=64)
+            nc.scalar.copy(
+                wg[:].rearrange("p (a i) j -> p a j i", i=RUN),
+                w_raw[c, h][:].rearrange("p j (a i) -> p a j i", i=RUN),
+            )
+            w_codes[c, h] = keep.tile([P, HALF], U32, name=f"wc{c}{h}", align_bytes=64)
+            w_scales[c, h] = keep.tile([P, HALF], U8, name=f"ws{c}{h}", align_bytes=64)
+            nc.vector.quantize_mx(
+                out=w_codes[c, h][:].bitcast(FP8X4),
+                scales=w_scales[c, h][:],
+                in_=wg[:].rearrange("p m j -> p (m j)"),
+            )
+
+        x_codes, x_scales = {}, {}
+        for c in range(PASSES):
+            picked = keep.tile([P, PACK, D, V], F32, name=f"picked{c}")
+            partial = keep.tile([P, PACK, V], F32, name=f"partial{c}")
+            for t in range(PACK):
+                last = c == PASSES - 1 and t == PACK - 1
+                cuts = [(0, 2), (2, 3)] if last else [(0, 3)]
+                for d0, d1 in cuts:
+                    nc.vector.tensor_tensor(
+                        picked[:, t, d0:d1, :].rearrange("p d v -> p (d v)"),
+                        planes[c, t][:].indirect(offsets[:, d0 * COLS : d1 * COLS]),
+                        gates[:, d0:d1, :].rearrange("p d v -> p (d v)"),
+                        MULT,
+                    )
+                nc.vector.tensor_tensor(partial[:, t, :], picked[:, t, 0, :], picked[:, t, 1, :], ADD)
+                if (c, t) == (1, 1):
+                    prepare_w(0, 0)
+                if (c, t) == (1, 2):
+                    prepare_w(0, 1)
+            grouped = keep.tile([P, V, PACK], BF16, name=f"xg{c}", align_bytes=64)
+            nc.vector.tensor_tensor(
+                grouped[:].rearrange("p (a i) t -> p a t i", i=RUN),
+                partial[:].rearrange("p t (a i) -> p a t i", i=RUN),
+                picked[:, :, 2, :].rearrange("p t (a i) -> p a t i", i=RUN),
+                ADD,
+            )
+            x_codes[c] = keep.tile([P, V], U32, name=f"xc{c}", align_bytes=64)
+            x_scales[c] = keep.tile([P, V], U8, name=f"xs{c}", align_bytes=64)
+            nc.vector.quantize_mx(
+                out=x_codes[c][:].bitcast(FP8X4),
+                scales=x_scales[c][:],
+                in_=grouped[:].rearrange("p v t -> p (v t)"),
+            )
+
+        accs = [psum.tile([P, V], F32, name=f"acc{mt}") for mt in range(N // P)]
+
+        def product(c, mt):
+            h, s = divmod(mt, HALF // P)
+            cols = slice(s * P, (s + 1) * P)
+            nc.tensor.matmul_mx(
+                out=accs[mt][:],
+                lhsT=w_codes[c, h][:, cols].bitcast(FP8X4),
+                lhsT_scale=w_scales[c, h][:, cols],
+                rhs=x_codes[c][:].bitcast(FP8X4),
+                rhs_scale=x_scales[c][:],
+                start=(c == 0),
+                stop=(c == PASSES - 1),
+            )
+
+        for mt in range(N // P):
+            product(0, mt)
+        for h in range(HALVES):
+            prepare_w(1, h)
+        for mt in range(N // P):
+            product(1, mt)
+            result = keep.tile([P, V], F32, name=f"res{mt}")
+            if mt % 2 == 0:
+                nc.scalar.activation(result[:], accs[mt][:], IDENT, bias=bias[:, mt : mt + 1])
+            else:
+                nc.vector.tensor_scalar(result[:], accs[mt][:], bias[:, mt : mt + 1], None, ADD)
+            nc.sync.dma_start(out[mt * P : (mt + 1) * P, :], result[:])

@@ -24,6 +24,7 @@ HALF = 256
 HALVES = N // HALF
 RUN = 4
 COLS = V // 16
+U = V // P
 
 
 def tile_picked_bag_lin_bias_sub_l_kernel(tc, xT, w, b, gate, offs, out):
@@ -31,17 +32,17 @@ def tile_picked_bag_lin_bias_sub_l_kernel(tc, xT, w, b, gate, offs, out):
     with ExitStack() as ctx:
         keep = ctx.enter_context(tc.tile_pool(name="keep", bufs=1))
         psum = ctx.enter_context(tc.psum_pool(name="psum", bufs=1))
+        ring = ctx.enter_context(tc.psum_pool(name="ring", bufs=2))
 
+        gate_cols = keep.tile([P, D, 8], F32, name="gate_cols")
+        nc.sync.dma_start(gate_cols[:, :, 0:U], gate[:, 0, :].rearrange("d (p e) -> p d e", e=U))
         offsets = keep.tile([P, D * COLS], U16, name="offsets")
         nc.sync.dma_start(offsets[:], offs)
-        gates = keep.tile([P, D, V], F32, name="gates")
-        nc.sync.dma_start(gates[:], gate.rearrange("d p v -> p d v"))
 
         x_rows = xT.rearrange("(c p t) n -> c t p n", p=P, t=PACK)
         w_rows = w.rearrange("(c p j) (h m) -> c h p j m", p=P, j=PACK, m=HALF)
         planes, w_raw = {}, {}
-        order = [("x", 0, 0), ("x", 0, 1), ("x", 0, 2), ("x", 0, 3), ("x", 1, 0), ("w", 0, 0), ("x", 1, 1),
-                 ("x", 1, 2), ("w", 0, 1), ("x", 1, 3), ("w", 1, 0), ("w", 1, 1)]
+        order = [("x", c, t) for c in range(PASSES) for t in range(PACK)] + [("w", c, h) for c in range(PASSES) for h in range(HALVES)]
         for kind, c, i in order:
             if kind == "x":
                 planes[c, i] = keep.tile([P, T], F32, name=f"plane{c}{i}")
@@ -52,56 +53,85 @@ def tile_picked_bag_lin_bias_sub_l_kernel(tc, xT, w, b, gate, offs, out):
 
         ident = keep.tile([P, P], F32, name="ident")
         make_identity(nc, ident[:])
+        gates = keep.tile([P, D, V], F32, name="gates")
+        for d0, d1, copy in ((0, 2, nc.vector.tensor_copy), (2, 3, nc.scalar.copy)):
+            spread = ring.tile([P, d1 - d0, U, P], F32, name="sums")
+            for d in range(d0, d1):
+                for e in range(U):
+                    nc.tensor.transpose(spread[:, d - d0, e, :], gate_cols[:, d, e : e + 1].to_broadcast([P, P]), ident[:])
+            copy(
+                gates[:, d0:d1, :].rearrange("p d (n e) -> p d n e", e=U),
+                spread[:].rearrange("p d e n -> p d n e"),
+            )
+        ident_bf = keep.tile([P, P], BF16, name="ident_bf")
+        nc.scalar.activation(ident_bf[:], ident[:], IDENT)
         bias_rows = keep.tile([P, P], F32, name="bias_rows")
         nc.gpsimd.memset(bias_rows[:], 0.0)
         nc.scalar.dma_start(bias_rows[0 : N // P, :], b.rearrange("(t p) o -> t (p o)", p=P))
-        bias_ps = psum.tile([P, P], F32, name="bias_ps")
-        nc.tensor.transpose(bias_ps[:], bias_rows[:], ident[:])
+        bias_ps = ring.tile([P, U, P], F32, name="sums")
+        nc.tensor.transpose(bias_ps[:, 0, :], bias_rows[:], ident[:])
         bias = keep.tile([P, 8], F32, name="bias")
-        nc.scalar.activation(bias[:], bias_ps[:, 0:8], IDENT)
+        nc.scalar.activation(bias[:], bias_ps[:, 0, 0:8], IDENT)
 
         w_codes, w_scales = {}, {}
 
-        def prepare_w(c, h):
-            wg = keep.tile([P, HALF, PACK], BF16, name=f"wg{c}{h}", align_bytes=64)
-            nc.scalar.copy(
-                wg[:].rearrange("p (a i) j -> p a j i", i=RUN),
-                w_raw[c, h][:].rearrange("p j (a i) -> p a j i", i=RUN),
-            )
+        def prepare_w(c, h, pieces):
             w_codes[c, h] = keep.tile([P, HALF], U32, name=f"wc{c}{h}", align_bytes=64)
             w_scales[c, h] = keep.tile([P, HALF], U8, name=f"ws{c}{h}", align_bytes=64)
-            nc.vector.quantize_mx(
-                out=w_codes[c, h][:].bitcast(FP8X4),
-                scales=w_scales[c, h][:],
-                in_=wg[:].rearrange("p m j -> p (m j)"),
-            )
+            width = HALF // len(pieces)
+            for n, copy in enumerate(pieces):
+                cols = slice(n * width, (n + 1) * width)
+                wg = keep.tile([P, width, PACK], BF16, name=f"wg{c}{h}{n}", align_bytes=64)
+                copy(
+                    wg[:].rearrange("p (a i) j -> p a j i", i=RUN),
+                    w_raw[c, h][:, :, cols].rearrange("p j (a i) -> p a j i", i=RUN),
+                )
+                nc.vector.quantize_mx(
+                    out=w_codes[c, h][:, cols].bitcast(FP8X4),
+                    scales=w_scales[c, h][:, cols],
+                    in_=wg[:].rearrange("p m j -> p (m j)"),
+                )
 
         x_codes, x_scales = {}, {}
         for c in range(PASSES):
-            picked = keep.tile([P, PACK, D, V], F32, name=f"picked{c}")
-            partial = keep.tile([P, PACK, V], F32, name=f"partial{c}")
+            back = [psum.tile([P, PACK, P], BF16, name=f"back{u}") for u in range(U)]
             for t in range(PACK):
                 last = c == PASSES - 1 and t == PACK - 1
-                cuts = [(0, 2), (2, 3)] if last else [(0, 3)]
-                for d0, d1 in cuts:
+                picked = keep.tile([P, D, V], F32, name=f"picked{c}{t}")
+                turned = keep.tile([P, U, P], BF16, name=f"turned{c}{t}")
+                if last:
+                    sums = [ring.tile([P, U, P], F32, name="sums") for u in range(U)]
+                    for d in range(D):
+                        nc.vector.tensor_tensor(
+                            picked[:, d, :],
+                            planes[c, t][:].indirect(offsets[:, d * COLS : (d + 1) * COLS]),
+                            gates[:, d, :],
+                            MULT,
+                        )
+                        for u in range(U):
+                            nc.tensor.matmul(sums[u][:, u, :], lhsT=picked[:, d, u * P : (u + 1) * P], rhs=ident[:],
+                                             start=(d == 0), stop=(d == D - 1), is_transpose=True)
+                    for u in range(U):
+                        nc.vector.tensor_copy(turned[:, u, :], sums[u][:, u, :])
+                else:
+                    sums = ring.tile([P, U, P], F32, name="sums")
                     nc.vector.tensor_tensor(
-                        picked[:, t, d0:d1, :].rearrange("p d v -> p (d v)"),
-                        planes[c, t][:].indirect(offsets[:, d0 * COLS : d1 * COLS]),
-                        gates[:, d0:d1, :].rearrange("p d v -> p (d v)"),
+                        picked[:].rearrange("p d v -> p (d v)"),
+                        planes[c, t][:].indirect(offsets[:]),
+                        gates[:].rearrange("p d v -> p (d v)"),
                         MULT,
                     )
-                nc.vector.tensor_tensor(partial[:, t, :], picked[:, t, 0, :], picked[:, t, 1, :], ADD)
-                if (c, t) == (1, 1):
-                    prepare_w(0, 0)
-                if (c, t) == (1, 2):
-                    prepare_w(0, 1)
+                    for u in range(U):
+                        for d in range(D):
+                            nc.tensor.matmul(sums[:, u, :], lhsT=picked[:, d, u * P : (u + 1) * P], rhs=ident[:],
+                                             start=(d == 0), stop=(d == D - 1), is_transpose=True)
+                    nc.scalar.copy(turned[:], sums[:])
+                for u in range(U):
+                    nc.tensor.transpose(back[u][:, t, :], turned[:, u, :], ident_bf[:])
             grouped = keep.tile([P, V, PACK], BF16, name=f"xg{c}", align_bytes=64)
-            nc.vector.tensor_tensor(
-                grouped[:].rearrange("p (a i) t -> p a t i", i=RUN),
-                partial[:].rearrange("p t (a i) -> p a t i", i=RUN),
-                picked[:, :, 2, :].rearrange("p t (a i) -> p a t i", i=RUN),
-                ADD,
-            )
+            for u in range(U):
+                copy = nc.scalar.copy if c == 0 else nc.vector.tensor_copy
+                copy(grouped[:, u * P : (u + 1) * P, :], back[u][:].rearrange("p t v -> p v t"))
             x_codes[c] = keep.tile([P, V], U32, name=f"xc{c}", align_bytes=64)
             x_scales[c] = keep.tile([P, V], U8, name=f"xs{c}", align_bytes=64)
             nc.vector.quantize_mx(
@@ -125,12 +155,14 @@ def tile_picked_bag_lin_bias_sub_l_kernel(tc, xT, w, b, gate, offs, out):
                 stop=(c == PASSES - 1),
             )
 
+        S, VV = nc.scalar.copy, nc.vector.tensor_copy
+        plan = {(0, 0): [S], (0, 1): [S], (1, 0): [S], (1, 1): [VV, S]}
+        for c in range(PASSES):
+            for h in range(HALVES):
+                prepare_w(c, h, plan[c, h])
+                for mt in range(h * 2, h * 2 + 2):
+                    product(c, mt)
         for mt in range(N // P):
-            product(0, mt)
-        for h in range(HALVES):
-            prepare_w(1, h)
-        for mt in range(N // P):
-            product(1, mt)
             result = keep.tile([P, V], F32, name=f"res{mt}")
             if mt % 2 == 0:
                 nc.scalar.activation(result[:], accs[mt][:], IDENT, bias=bias[:, mt : mt + 1])

@@ -21,10 +21,12 @@ PACK = 4
 K_PASS = P * PACK
 PASSES = K // K_PASS
 HALF = 256
-HALVES = N // HALF
 RUN = 4
 COLS = V // 16
 U = V // P
+QUAD = 32
+ROW_STEP = D * P // QUAD
+M_TILES = N // P
 
 
 def tile_picked_bag_lin_bias_sub_l_kernel(tc, xT, w, b, gate, offs, out):
@@ -32,140 +34,178 @@ def tile_picked_bag_lin_bias_sub_l_kernel(tc, xT, w, b, gate, offs, out):
     with ExitStack() as ctx:
         keep = ctx.enter_context(tc.tile_pool(name="keep", bufs=1))
         psum = ctx.enter_context(tc.psum_pool(name="psum", bufs=1))
-        ring = ctx.enter_context(tc.psum_pool(name="ring", bufs=2))
-
-        gate_cols = keep.tile([P, D, 8], F32, name="gate_cols")
-        nc.sync.dma_start(gate_cols[:, :, 0:U], gate[:, 0, :].rearrange("d (p e) -> p d e", e=U))
-        offsets = keep.tile([P, D * COLS], U16, name="offsets")
-        nc.sync.dma_start(offsets[:], offs)
+        ring = ctx.enter_context(tc.psum_pool(name="ring", bufs=3))
 
         x_rows = xT.rearrange("(c p t) n -> c t p n", p=P, t=PACK)
-        w_rows = w.rearrange("(c p j) (h m) -> c h p j m", p=P, j=PACK, m=HALF)
+        w_rows = w.rearrange("(c p j) m -> c p j m", p=P, j=PACK)
+        rows = keep.tile([P, V], F32, name="rows")
+        gate_rows = gate.rearrange("d p v -> (d p) v").rearrange("(r s) v -> r s v", s=ROW_STEP)
+        nc.sync.dma_start(rows[0:QUAD, :], gate_rows[:, 0, :])
+        offsets = keep.tile([P, D * COLS], U16, name="offsets")
         planes, w_raw = {}, {}
-        order = [("x", c, t) for c in range(PASSES) for t in range(PACK)] + [("w", c, h) for c in range(PASSES) for h in range(HALVES)]
-        for kind, c, i in order:
+        for kind, c, m0, m1 in [("x", 0, 0, 0), ("x", 0, 1, 0), ("x", 0, 2, 0), ("x", 0, 3, 0), ("x", 1, 0, 0), ("x", 1, 1, 0), ("x", 1, 2, 0), ("x", 1, 3, 0), ("w", 0, 0, 512), ("w", 1, 0, 256), ("w", 1, 256, 512)]:
             if kind == "x":
-                planes[c, i] = keep.tile([P, T], F32, name=f"plane{c}{i}")
-                nc.sync.dma_start(planes[c, i][:], x_rows[c, i])
+                planes[c, m0] = keep.tile([P, T], F32, name=f"plane{c}{m0}")
+                nc.sync.dma_start(planes[c, m0][:], x_rows[c, m0])
+                if (c, m0) == (0, 0):
+                    nc.sync.dma_start(offsets[:], offs)
             else:
-                w_raw[c, i] = keep.tile([P, PACK, HALF], F32, name=f"wraw{c}{i}")
-                nc.sync.dma_start(w_raw[c, i][:], w_rows[c, i])
+                raw = keep.tile([P, PACK, m1 - m0], F32, name=f"wraw{c}_{m0}")
+                nc.sync.dma_start(raw[:], w_rows[c, :, :, m0:m1])
+                for mt in range(m0 // P, m1 // P):
+                    w_raw[c, mt] = (raw, m0)
 
+        nc.vector.memset(rows[QUAD : 2 * QUAD, :], 0.0)
+        nc.vector.memset(rows[2 * QUAD : P, :], 0.0)
         ident = keep.tile([P, P], F32, name="ident")
         make_identity(nc, ident[:])
-        gates = keep.tile([P, D, V], F32, name="gates")
-        for d0, d1, copy in ((0, 2, nc.vector.tensor_copy), (2, 3, nc.scalar.copy)):
-            spread = ring.tile([P, d1 - d0, U, P], F32, name="sums")
-            for d in range(d0, d1):
-                for e in range(U):
-                    nc.tensor.transpose(spread[:, d - d0, e, :], gate_cols[:, d, e : e + 1].to_broadcast([P, P]), ident[:])
-            copy(
-                gates[:, d0:d1, :].rearrange("p d (n e) -> p d n e", e=U),
-                spread[:].rearrange("p d e n -> p d n e"),
-            )
         ident_bf = keep.tile([P, P], BF16, name="ident_bf")
         nc.scalar.activation(ident_bf[:], ident[:], IDENT)
+        upright = ring.tile([P, U, P], F32, name="sums")
+        for u in range(U):
+            nc.tensor.transpose(upright[:, u, :], rows[:, u * P : (u + 1) * P], ident[:])
+        columns = keep.tile([P, U, QUAD], F32, name="columns")
+        nc.vector.tensor_copy(columns[:], upright[:, :, 0:QUAD])
+        gates = keep.tile([P, D, V], F32, name="gates")
+        for d0, d1, copy in ((0, 2, nc.vector.tensor_copy), (2, 3, nc.scalar.copy)):
+            spread = ring.tile([P, d1 - d0, V], F32, name="sums")
+            for d in range(d0, d1):
+                r = -(-d * P // ROW_STEP)
+                for u in range(U):
+                    nc.tensor.transpose(
+                        spread[:, d - d0, u * P : (u + 1) * P], columns[:, u, r : r + 1].to_broadcast([P, P]), ident[:]
+                    )
+            copy(gates[:, d0:d1, :], spread[:])
+
         bias_rows = keep.tile([P, P], F32, name="bias_rows")
         nc.gpsimd.memset(bias_rows[:], 0.0)
-        nc.scalar.dma_start(bias_rows[0 : N // P, :], b.rearrange("(t p) o -> t (p o)", p=P))
-        bias_ps = ring.tile([P, U, P], F32, name="sums")
-        nc.tensor.transpose(bias_ps[:, 0, :], bias_rows[:], ident[:])
+        nc.scalar.dma_start(bias_rows[0:M_TILES, :], b.rearrange("(t p) o -> t (p o)", p=P))
+        bias_ps = ring.tile([P, P], F32, name="sums")
+        nc.tensor.transpose(bias_ps[:], bias_rows[:], ident[:])
         bias = keep.tile([P, 8], F32, name="bias")
-        nc.scalar.activation(bias[:], bias_ps[:, 0, 0:8], IDENT)
+        nc.scalar.copy(bias[:], bias_ps[:, 0:8])
 
-        w_codes, w_scales = {}, {}
+        w_codes = [keep.tile([P, N], U32, name=f"wc{c}", align_bytes=64) for c in range(PASSES)]
+        w_scales = [keep.tile([P, N], U8, name=f"ws{c}", align_bytes=64) for c in range(PASSES)]
+        w_grouped = {}
 
-        def prepare_w(c, h, pieces):
-            w_codes[c, h] = keep.tile([P, HALF], U32, name=f"wc{c}{h}", align_bytes=64)
-            w_scales[c, h] = keep.tile([P, HALF], U8, name=f"ws{c}{h}", align_bytes=64)
-            width = HALF // len(pieces)
-            for n, copy in enumerate(pieces):
-                cols = slice(n * width, (n + 1) * width)
-                wg = keep.tile([P, width, PACK], BF16, name=f"wg{c}{h}{n}", align_bytes=64)
-                copy(
-                    wg[:].rearrange("p (a i) j -> p a j i", i=RUN),
-                    w_raw[c, h][:, :, cols].rearrange("p j (a i) -> p a j i", i=RUN),
-                )
-                nc.vector.quantize_mx(
-                    out=w_codes[c, h][:, cols].bitcast(FP8X4),
-                    scales=w_scales[c, h][:, cols],
-                    in_=wg[:].rearrange("p m j -> p (m j)"),
-                )
+        def round_w(c, m0, m1, copy):
+            raw, base = w_raw[c, m0 // P]
+            w_grouped[c, m0] = keep.tile([P, m1 - m0, PACK], BF16, name=f"wg{c}_{m0}", align_bytes=64)
+            copy(
+                w_grouped[c, m0][:].rearrange("p (a i) j -> p a j i", i=RUN),
+                raw[:, :, m0 - base : m1 - base].rearrange("p j (a i) -> p a j i", i=RUN),
+            )
 
-        x_codes, x_scales = {}, {}
-        for c in range(PASSES):
-            back = [psum.tile([P, PACK, P], BF16, name=f"back{u}") for u in range(U)]
-            for t in range(PACK):
-                last = c == PASSES - 1 and t == PACK - 1
-                picked = keep.tile([P, D, V], F32, name=f"picked{c}{t}")
-                turned = keep.tile([P, U, P], BF16, name=f"turned{c}{t}")
-                if last:
-                    sums = [ring.tile([P, U, P], F32, name="sums") for u in range(U)]
-                    for d in range(D):
-                        nc.vector.tensor_tensor(
-                            picked[:, d, :],
-                            planes[c, t][:].indirect(offsets[:, d * COLS : (d + 1) * COLS]),
-                            gates[:, d, :],
-                            MULT,
-                        )
-                        for u in range(U):
-                            nc.tensor.matmul(sums[u][:, u, :], lhsT=picked[:, d, u * P : (u + 1) * P], rhs=ident[:],
-                                             start=(d == 0), stop=(d == D - 1), is_transpose=True)
-                    for u in range(U):
-                        nc.vector.tensor_copy(turned[:, u, :], sums[u][:, u, :])
-                else:
-                    sums = ring.tile([P, U, P], F32, name="sums")
-                    nc.vector.tensor_tensor(
-                        picked[:].rearrange("p d v -> p (d v)"),
-                        planes[c, t][:].indirect(offsets[:]),
-                        gates[:].rearrange("p d v -> p (d v)"),
-                        MULT,
-                    )
-                    for u in range(U):
-                        for d in range(D):
-                            nc.tensor.matmul(sums[:, u, :], lhsT=picked[:, d, u * P : (u + 1) * P], rhs=ident[:],
-                                             start=(d == 0), stop=(d == D - 1), is_transpose=True)
-                    nc.scalar.copy(turned[:], sums[:])
-                for u in range(U):
-                    nc.tensor.transpose(back[u][:, t, :], turned[:, u, :], ident_bf[:])
-            grouped = keep.tile([P, V, PACK], BF16, name=f"xg{c}", align_bytes=64)
+        def quantize_w(c, m0, m1):
+            nc.vector.quantize_mx(
+                out=w_codes[c][:, m0:m1].bitcast(FP8X4),
+                scales=w_scales[c][:, m0:m1],
+                in_=w_grouped[c, m0][:].rearrange("p m j -> p (m j)"),
+            )
+
+        def gather(picked, c, t, d0, d1):
+            nc.vector.tensor_tensor(
+                picked[:, d0:d1, :].rearrange("p d v -> p (d v)"),
+                planes[c, t][:].indirect(offsets[:, d0 * COLS : d1 * COLS]),
+                gates[:, d0:d1, :].rearrange("p d v -> p (d v)"),
+                MULT,
+            )
+
+        def sum_on_tensor(c, t, back):
+            picked = keep.tile([P, D, V], F32, name=f"picked{c}{t}")
+            gather(picked, c, t, 0, D)
+            sums = ring.tile([P, U, P], F32, name="sums")
             for u in range(U):
-                copy = nc.scalar.copy if c == 0 else nc.vector.tensor_copy
-                copy(grouped[:, u * P : (u + 1) * P, :], back[u][:].rearrange("p t v -> p v t"))
-            x_codes[c] = keep.tile([P, V], U32, name=f"xc{c}", align_bytes=64)
-            x_scales[c] = keep.tile([P, V], U8, name=f"xs{c}", align_bytes=64)
+                for d in range(D):
+                    nc.tensor.matmul(sums[:, u, :], lhsT=picked[:, d, u * P : (u + 1) * P], rhs=ident[:],
+                                     start=(d == 0), stop=(d == D - 1), is_transpose=True)
+            turned = keep.tile([P, U, P], BF16, name=f"turned{c}{t}")
+            nc.scalar.copy(turned[:], sums[:])
+            for u in range(U):
+                nc.tensor.transpose(back[:, t, u * P : (u + 1) * P], turned[:, u, :], ident_bf[:])
+
+        x_codes = [keep.tile([P, V], U32, name=f"xc{c}", align_bytes=64) for c in range(PASSES)]
+        x_scales = [keep.tile([P, V], U8, name=f"xs{c}", align_bytes=64) for c in range(PASSES)]
+        x_grouped = [keep.tile([P, V, PACK], BF16, name=f"xg{c}", align_bytes=64) for c in range(PASSES)]
+
+        def quantize_x(c):
             nc.vector.quantize_mx(
                 out=x_codes[c][:].bitcast(FP8X4),
                 scales=x_scales[c][:],
-                in_=grouped[:].rearrange("p v t -> p (v t)"),
+                in_=x_grouped[c][:].rearrange("p v t -> p (v t)"),
             )
 
-        accs = [psum.tile([P, V], F32, name=f"acc{mt}") for mt in range(N // P)]
+        accs = [psum.tile([P, V], F32, name=f"acc{mt}") for mt in range(M_TILES)]
 
         def product(c, mt):
-            h, s = divmod(mt, HALF // P)
-            cols = slice(s * P, (s + 1) * P)
+            cols = slice(mt * P, (mt + 1) * P)
             nc.tensor.matmul_mx(
                 out=accs[mt][:],
-                lhsT=w_codes[c, h][:, cols].bitcast(FP8X4),
-                lhsT_scale=w_scales[c, h][:, cols],
+                lhsT=w_codes[c][:, cols].bitcast(FP8X4),
+                lhsT_scale=w_scales[c][:, cols],
                 rhs=x_codes[c][:].bitcast(FP8X4),
                 rhs_scale=x_scales[c][:],
                 start=(c == 0),
                 stop=(c == PASSES - 1),
             )
 
-        S, VV = nc.scalar.copy, nc.vector.tensor_copy
-        plan = {(0, 0): [S], (0, 1): [S], (1, 0): [S], (1, 1): [VV, S]}
-        for c in range(PASSES):
-            for h in range(HALVES):
-                prepare_w(c, h, plan[c, h])
-                for mt in range(h * 2, h * 2 + 2):
-                    product(c, mt)
-        for mt in range(N // P):
+        def finish(mt, on_scalar):
             result = keep.tile([P, V], F32, name=f"res{mt}")
-            if mt % 2 == 0:
+            if on_scalar:
                 nc.scalar.activation(result[:], accs[mt][:], IDENT, bias=bias[:, mt : mt + 1])
             else:
                 nc.vector.tensor_scalar(result[:], accs[mt][:], bias[:, mt : mt + 1], None, ADD)
             nc.sync.dma_start(out[mt * P : (mt + 1) * P, :], result[:])
+
+        S, VV = nc.scalar.copy, nc.vector.tensor_copy
+
+        back = psum.tile([P, PACK, V], BF16, name="back")
+        for t in range(PACK):
+            sum_on_tensor(0, t, back)
+        nc.scalar.copy(x_grouped[0][:], back[:].rearrange("p t v -> p v t"))
+        quantize_x(0)
+
+        back = psum.tile([P, PACK, V], BF16, name="back")
+        flat = keep.tile([P, PACK, V], BF16, name="flat")
+        for t in range(PACK - 1):
+            sum_on_tensor(1, t, back)
+            nc.scalar.copy(flat[:, t, :], back[:, t, :])
+        picked = keep.tile([P, D, V], F32, name="picked_last")
+        partial = keep.tile([P, V], F32, name="partial")
+        gather(picked, 1, PACK - 1, 0, 2)
+        gather(picked, 1, PACK - 1, 2, 3)
+        nc.vector.tensor_tensor(partial[:], picked[:, 0, :], picked[:, 1, :], ADD)
+        nc.vector.tensor_tensor(flat[:, PACK - 1, :], partial[:], picked[:, 2, :], ADD)
+
+        def interleave_x():
+            nc.vector.tensor_copy(
+                x_grouped[1][:].rearrange("p (a i) t -> p a t i", i=RUN),
+                flat[:].rearrange("p t (a i) -> p a t i", i=RUN),
+            )
+
+        idle = ring.tile([P, PACK, P], F32, name="sums")
+        for n in range(8):
+            nc.tensor.transpose(idle[:, n % PACK, :], picked[:, n % 2, 0:P], ident[:])
+        for n in range(8):
+            nc.tensor.transpose(idle[:, n % PACK, :], partial[:, 0:P], ident[:])
+        round_w(0, 0, 256, S)
+        round_w(0, 256, 512, VV)
+        quantize_w(0, 0, 256)
+        interleave_x()
+        quantize_w(0, 256, 512)
+        quantize_x(1)
+        for mt in range(M_TILES):
+            product(0, mt)
+        round_w(1, 0, 256, S)
+        quantize_w(1, 0, 256)
+        product(1, 0)
+        product(1, 1)
+        round_w(1, 256, 384, S)
+        round_w(1, 384, 512, S)
+        quantize_w(1, 256, 384)
+        quantize_w(1, 384, 512)
+        product(1, 2)
+        product(1, 3)
+        for mt, on_scalar in enumerate((True, True, False, True)):
+            finish(mt, on_scalar)

@@ -45,7 +45,7 @@ def tile_picked_bag_lin_bias_sub_l_kernel(tc, xT, w, b, gate, offs, out):
         planes, w_raw = {}, {}
         for kind, c, m0, m1 in [("x", 0, 0, 0), ("x", 0, 1, 0), ("x", 0, 2, 0), ("x", 0, 3, 0), ("x", 1, 0, 0), ("x", 1, 1, 0), ("x", 1, 2, 0), ("x", 1, 3, 0), ("w", 0, 0, 512), ("w", 1, 0, 256), ("w", 1, 256, 512)]:
             if kind == "x":
-                planes[c, m0] = keep.tile([P, T], F32, name=f"plane{c}{m0}")
+                planes[c, m0] = keep.tile([P, T], F32, name=f"plane{c}{m0}", tag=f"plane{c}{m0}", align_bytes=64)
                 nc.sync.dma_start(planes[c, m0][:], x_rows[c, m0])
                 if (c, m0) == (0, 0):
                     nc.sync.dma_start(offsets[:], offs)
@@ -80,10 +80,7 @@ def tile_picked_bag_lin_bias_sub_l_kernel(tc, xT, w, b, gate, offs, out):
         bias_rows = keep.tile([P, P], F32, name="bias_rows")
         nc.gpsimd.memset(bias_rows[:], 0.0)
         nc.scalar.dma_start(bias_rows[0:M_TILES, :], b.rearrange("(t p) o -> t (p o)", p=P))
-        bias_ps = ring.tile([P, P], F32, name="sums")
-        nc.tensor.transpose(bias_ps[:], bias_rows[:], ident[:])
         bias = keep.tile([P, 8], F32, name="bias")
-        nc.scalar.copy(bias[:], bias_ps[:, 0:8])
 
         w_codes = [keep.tile([P, N], U32, name=f"wc{c}", align_bytes=64) for c in range(PASSES)]
         w_scales = [keep.tile([P, N], U8, name=f"ws{c}", align_bytes=64) for c in range(PASSES)]
@@ -125,11 +122,12 @@ def tile_picked_bag_lin_bias_sub_l_kernel(tc, xT, w, b, gate, offs, out):
             for u in range(U):
                 nc.tensor.transpose(back[:, t, u * P : (u + 1) * P], turned[:, u, :], ident_bf[:])
 
-        x_codes = [keep.tile([P, V], U32, name=f"xc{c}", align_bytes=64) for c in range(PASSES)]
+        x_codes = {}
         x_scales = [keep.tile([P, V], U8, name=f"xs{c}", align_bytes=64) for c in range(PASSES)]
         x_grouped = [keep.tile([P, V, PACK], BF16, name=f"xg{c}", align_bytes=64) for c in range(PASSES)]
 
         def quantize_x(c):
+            x_codes[c] = keep.tile([P, V], U32, name=f"xc{c}", tag=("plane11" if c == 0 else "xc1"), align_bytes=64)
             nc.vector.quantize_mx(
                 out=x_codes[c][:].bitcast(FP8X4),
                 scales=x_scales[c][:],
@@ -156,7 +154,8 @@ def tile_picked_bag_lin_bias_sub_l_kernel(tc, xT, w, b, gate, offs, out):
                 nc.scalar.activation(result[:], accs[mt][:], IDENT, bias=bias[:, mt : mt + 1])
             else:
                 nc.vector.tensor_scalar(result[:], accs[mt][:], bias[:, mt : mt + 1], None, ADD)
-            nc.sync.dma_start(out[mt * P : (mt + 1) * P, :], result[:])
+            queue = nc.scalar if mt == M_TILES - 1 else nc.sync
+            queue.dma_start(out[mt * P : (mt + 1) * P, :], result[:])
 
         S, VV = nc.scalar.copy, nc.vector.tensor_copy
 
@@ -164,13 +163,17 @@ def tile_picked_bag_lin_bias_sub_l_kernel(tc, xT, w, b, gate, offs, out):
         for t in range(PACK):
             sum_on_tensor(0, t, back)
         nc.scalar.copy(x_grouped[0][:], back[:].rearrange("p t v -> p v t"))
-        quantize_x(0)
+        bias_ps = ring.tile([P, P], F32, name="sums")
+        nc.tensor.transpose(bias_ps[:], bias_rows[:], ident[:])
+        nc.scalar.copy(bias[:], bias_ps[:, 0:8])
 
         back = psum.tile([P, PACK, V], BF16, name="back")
         flat = keep.tile([P, PACK, V], BF16, name="flat")
         for t in range(PACK - 1):
             sum_on_tensor(1, t, back)
             nc.scalar.copy(flat[:, t, :], back[:, t, :])
+            if t == 1:
+                quantize_x(0)
         picked = keep.tile([P, D, V], F32, name="picked_last")
         partial = keep.tile([P, V], F32, name="partial")
         gather(picked, 1, PACK - 1, 0, 2)
@@ -202,7 +205,7 @@ def tile_picked_bag_lin_bias_sub_l_kernel(tc, xT, w, b, gate, offs, out):
         product(1, 0)
         product(1, 1)
         round_w(1, 256, 384, S)
-        round_w(1, 384, 512, S)
+        round_w(1, 384, 512, VV)
         quantize_w(1, 256, 384)
         quantize_w(1, 384, 512)
         product(1, 2)

@@ -24,8 +24,6 @@ HALF = 256
 RUN = 4
 COLS = V // 16
 U = V // P
-QUAD = 32
-ROW_STEP = D * P // QUAD
 M_TILES = N // P
 
 
@@ -38,44 +36,47 @@ def tile_picked_bag_lin_bias_sub_l_kernel(tc, xT, w, b, gate, offs, out):
 
         x_rows = xT.rearrange("(c p t) n -> c t p n", p=P, t=PACK)
         w_rows = w.rearrange("(c p j) m -> c p j m", p=P, j=PACK)
-        rows = keep.tile([P, V], F32, name="rows")
-        gate_rows = gate.rearrange("d p v -> (d p) v").rearrange("(r s) v -> r s v", s=ROW_STEP)
-        nc.sync.dma_start(rows[0:QUAD, :], gate_rows[:, 0, :])
         offsets = keep.tile([P, D * COLS], U16, name="offsets")
+        columns = keep.tile([P, D, U], F32, name="columns")
+        nc.sync.dma_start(columns[:], gate[:, 0, :].rearrange("d (p u) -> p d u", u=U))
         planes, w_raw = {}, {}
-        for kind, c, m0, m1 in [("x", 0, 0, 0), ("x", 0, 1, 0), ("x", 0, 2, 0), ("x", 0, 3, 0), ("x", 1, 0, 0), ("x", 1, 1, 0), ("x", 1, 2, 0), ("x", 1, 3, 0), ("w", 0, 0, 512), ("w", 1, 0, 256), ("w", 1, 256, 512)]:
-            if kind == "x":
-                planes[c, m0] = keep.tile([P, T], F32, name=f"plane{c}{m0}", tag=f"plane{c}{m0}", align_bytes=64)
-                nc.sync.dma_start(planes[c, m0][:], x_rows[c, m0])
-                if (c, m0) == (0, 0):
-                    nc.sync.dma_start(offsets[:], offs)
-            else:
-                raw = keep.tile([P, PACK, m1 - m0], F32, name=f"wraw{c}_{m0}")
-                nc.sync.dma_start(raw[:], w_rows[c, :, :, m0:m1])
-                for mt in range(m0 // P, m1 // P):
-                    w_raw[c, mt] = (raw, m0)
+        shared = keep.tile([P, V + PACK * HALF], F32, name="shared")
 
-        nc.vector.memset(rows[QUAD : 2 * QUAD, :], 0.0)
-        nc.vector.memset(rows[2 * QUAD : P, :], 0.0)
+        def load_w(c, h):
+            if (c, h) == (0, 0):
+                w_raw[c, h] = shared[:, V : V + PACK * HALF].rearrange("p (j m) -> p j m", j=PACK)
+            else:
+                raw = keep.tile([P, PACK, HALF], F32, name=f"wraw{c}{h}")
+                w_raw[c, h] = raw[:]
+            nc.sync.dma_start(w_raw[c, h], w_rows[c, :, :, h * HALF : (h + 1) * HALF])
+
+        for c in range(PASSES):
+            for t in range(PACK):
+                planes[c, t] = keep.tile([P, T], F32, name=f"plane{c}{t}", tag=f"plane{c}{t}", align_bytes=64)
+                nc.sync.dma_start(planes[c, t][:], x_rows[c, t])
+                if (c, t) == (0, 0):
+                    nc.sync.dma_start(offsets[:], offs)
+        load_w(0, 0)
+        load_w(0, 1)
+        load_w(1, 0)
+        load_w(1, 1)
+
         ident = keep.tile([P, P], F32, name="ident")
         make_identity(nc, ident[:])
         ident_bf = keep.tile([P, P], BF16, name="ident_bf")
         nc.scalar.activation(ident_bf[:], ident[:], IDENT)
-        upright = ring.tile([P, U, P], F32, name="sums")
-        for u in range(U):
-            nc.tensor.transpose(upright[:, u, :], rows[:, u * P : (u + 1) * P], ident[:])
-        columns = keep.tile([P, U, QUAD], F32, name="columns")
-        nc.vector.tensor_copy(columns[:], upright[:, :, 0:QUAD])
         gates = keep.tile([P, D, V], F32, name="gates")
-        for d0, d1, copy in ((0, 2, nc.vector.tensor_copy), (2, 3, nc.scalar.copy)):
-            spread = ring.tile([P, d1 - d0, V], F32, name="sums")
+        for d0, d1 in ((0, 2), (2, 3)):
+            spread = ring.tile([P, d1 - d0, U, P], F32, name="sums")
             for d in range(d0, d1):
-                r = -(-d * P // ROW_STEP)
                 for u in range(U):
                     nc.tensor.transpose(
-                        spread[:, d - d0, u * P : (u + 1) * P], columns[:, u, r : r + 1].to_broadcast([P, P]), ident[:]
+                        spread[:, d - d0, u, :], columns[:, d, u : u + 1].to_broadcast([P, P]), ident[:]
                     )
-            copy(gates[:, d0:d1, :], spread[:])
+            nc.scalar.copy(
+                gates[:, d0:d1, :].rearrange("q d (p u) -> q d p u", u=U),
+                spread[:].rearrange("q d u p -> q d p u"),
+            )
 
         bias_rows = keep.tile([P, P], F32, name="bias_rows")
         nc.gpsimd.memset(bias_rows[:], 0.0)
@@ -84,21 +85,19 @@ def tile_picked_bag_lin_bias_sub_l_kernel(tc, xT, w, b, gate, offs, out):
 
         w_codes = [keep.tile([P, N], U32, name=f"wc{c}", align_bytes=64) for c in range(PASSES)]
         w_scales = [keep.tile([P, N], U8, name=f"ws{c}", align_bytes=64) for c in range(PASSES)]
-        w_grouped = {}
+        w_grouped = [keep.tile([P, N, PACK], BF16, name=f"wg{c}", align_bytes=64) for c in range(PASSES)]
 
         def round_w(c, m0, m1, copy):
-            raw, base = w_raw[c, m0 // P]
-            w_grouped[c, m0] = keep.tile([P, m1 - m0, PACK], BF16, name=f"wg{c}_{m0}", align_bytes=64)
             copy(
-                w_grouped[c, m0][:].rearrange("p (a i) j -> p a j i", i=RUN),
-                raw[:, :, m0 - base : m1 - base].rearrange("p j (a i) -> p a j i", i=RUN),
+                w_grouped[c][:, m0:m1, :].rearrange("p (a i) j -> p a j i", i=RUN),
+                w_raw[c, m0 // HALF][:, :, m0 % HALF : m0 % HALF + m1 - m0].rearrange("p j (a i) -> p a j i", i=RUN),
             )
 
         def quantize_w(c, m0, m1):
             nc.vector.quantize_mx(
                 out=w_codes[c][:, m0:m1].bitcast(FP8X4),
                 scales=w_scales[c][:, m0:m1],
-                in_=w_grouped[c, m0][:].rearrange("p m j -> p (m j)"),
+                in_=w_grouped[c][:, m0:m1, :].rearrange("p m j -> p (m j)"),
             )
 
         def gather(picked, c, t, d0, d1):
@@ -168,9 +167,11 @@ def tile_picked_bag_lin_bias_sub_l_kernel(tc, xT, w, b, gate, offs, out):
         nc.scalar.copy(bias[:], bias_ps[:, 0:8])
 
         back = psum.tile([P, PACK, V], BF16, name="back")
-        flat = keep.tile([P, PACK, V], BF16, name="flat")
+        flat = shared[:, 0 : PACK * V // 2].bitcast(BF16).rearrange("p (t v) -> p t v", t=PACK)
         for t in range(PACK - 1):
             sum_on_tensor(1, t, back)
+            if t == PACK - 2:
+                round_w(0, 0, 256, S)
             nc.scalar.copy(flat[:, t, :], back[:, t, :])
             if t == 1:
                 quantize_x(0)
@@ -179,32 +180,27 @@ def tile_picked_bag_lin_bias_sub_l_kernel(tc, xT, w, b, gate, offs, out):
         gather(picked, 1, PACK - 1, 0, 2)
         gather(picked, 1, PACK - 1, 2, 3)
         nc.vector.tensor_tensor(partial[:], picked[:, 0, :], picked[:, 1, :], ADD)
+        round_w(0, 384, 512, VV)
         nc.vector.tensor_tensor(flat[:, PACK - 1, :], partial[:], picked[:, 2, :], ADD)
 
         def interleave_x():
             nc.vector.tensor_copy(
                 x_grouped[1][:].rearrange("p (a i) t -> p a t i", i=RUN),
-                flat[:].rearrange("p t (a i) -> p a t i", i=RUN),
+                flat.rearrange("p t (a i) -> p a t i", i=RUN),
             )
 
-        idle = ring.tile([P, PACK, P], F32, name="sums")
-        for n in range(8):
-            nc.tensor.transpose(idle[:, n % PACK, :], picked[:, n % 2, 0:P], ident[:])
-        for n in range(8):
-            nc.tensor.transpose(idle[:, n % PACK, :], partial[:, 0:P], ident[:])
-        round_w(0, 0, 256, S)
-        round_w(0, 256, 512, VV)
+        round_w(0, 256, 384, S)
+        round_w(1, 0, 256, S)
+        round_w(1, 256, 384, S)
         quantize_w(0, 0, 256)
         interleave_x()
         quantize_w(0, 256, 512)
         quantize_x(1)
         for mt in range(M_TILES):
             product(0, mt)
-        round_w(1, 0, 256, S)
         quantize_w(1, 0, 256)
         product(1, 0)
         product(1, 1)
-        round_w(1, 256, 384, S)
         round_w(1, 384, 512, VV)
         quantize_w(1, 256, 384)
         quantize_w(1, 384, 512)

@@ -22,6 +22,8 @@ K_PASS = P * PACK
 PASSES = K // K_PASS
 HALF = 256
 RUN = 4
+QUAD = 32
+DEAL = 8
 COLS = V // 16
 U = V // P
 M_TILES = N // P
@@ -37,8 +39,12 @@ def tile_picked_bag_lin_bias_sub_l_kernel(tc, xT, w, b, gate, offs, out):
         x_rows = xT.rearrange("(c p t) n -> c t p n", p=P, t=PACK)
         w_rows = w.rearrange("(c p j) m -> c p j m", p=P, j=PACK)
         offsets = keep.tile([P, D * COLS], U16, name="offsets")
-        columns = keep.tile([P, D, U], F32, name="columns")
-        nc.sync.dma_start(columns[:], gate[:, 0, :].rearrange("d (p u) -> p d u", u=U))
+        columns = keep.tile([P, DEAL], F32, name="columns")
+        gate_flat = gate.rearrange("d p v -> (d p v)")
+        first = (P - 1) * V
+        nc.scalar.dma_start(columns[0 : 2 * QUAD, :], gate_flat[first : first + 2 * V].rearrange("(p i) -> p i", i=DEAL))
+        nc.scalar.dma_start(columns[2 * QUAD : 3 * QUAD, :], gate[2, 0, :].rearrange("(p i) -> p i", i=DEAL))
+        nc.vector.memset(columns[3 * QUAD : P, :], 0.0)
         planes, w_raw = {}, {}
         shared = keep.tile([P, V + PACK * HALF], F32, name="shared")
 
@@ -66,17 +72,12 @@ def tile_picked_bag_lin_bias_sub_l_kernel(tc, xT, w, b, gate, offs, out):
         ident_bf = keep.tile([P, P], BF16, name="ident_bf")
         nc.scalar.activation(ident_bf[:], ident[:], IDENT)
         gates = keep.tile([P, D, V], F32, name="gates")
-        for d0, d1 in ((0, 2), (2, 3)):
-            spread = ring.tile([P, d1 - d0, U, P], F32, name="sums")
-            for d in range(d0, d1):
-                for u in range(U):
-                    nc.tensor.transpose(
-                        spread[:, d - d0, u, :], columns[:, d, u : u + 1].to_broadcast([P, P]), ident[:]
-                    )
-            nc.scalar.copy(
-                gates[:, d0:d1, :].rearrange("q d (p u) -> q d p u", u=U),
-                spread[:].rearrange("q d u p -> q d p u"),
-            )
+        dealt = gates[:].rearrange("q d v -> q (d v)").rearrange("q (p i) -> q p i", i=DEAL)
+        for i0, copy in ((0, nc.vector.tensor_copy), (PACK, nc.scalar.copy)):
+            spread = ring.tile([P, PACK, P], F32, name="sums")
+            for i in range(PACK):
+                nc.tensor.transpose(spread[:, i, :], columns[:, i0 + i : i0 + i + 1].to_broadcast([P, P]), ident[:])
+            copy(dealt[:, :, i0 : i0 + PACK], spread[:, :, 0 : 3 * QUAD].rearrange("q i p -> q p i"))
 
         bias_rows = keep.tile([P, P], F32, name="bias_rows")
         nc.gpsimd.memset(bias_rows[:], 0.0)

@@ -9,6 +9,7 @@ FLOPS = 2 * K * N * V
 F32 = mybir.dt.float32
 BF16 = mybir.dt.bfloat16
 U32 = mybir.dt.uint32
+I32 = mybir.dt.int32
 U16 = mybir.dt.uint16
 U8 = mybir.dt.uint8
 FP8X4 = mybir.dt.float8_e4m3fn_x4
@@ -18,15 +19,16 @@ IDENT = mybir.ActivationFunctionType.Identity
 
 P = 128
 PACK = 4
-K_PASS = P * PACK
-PASSES = K // K_PASS
-HALF = 256
+PAIR = 2
+PASSES = K // (P * PACK)
+HALF = N // 2
 RUN = 4
 QUAD = 32
 DEAL = 8
 COLS = V // 16
 U = V // P
 M_TILES = N // P
+SUM_BANKS = 3
 
 
 def tile_picked_bag_lin_bias_sub_l_kernel(tc, xT, w, b, gate, offs, out):
@@ -34,17 +36,19 @@ def tile_picked_bag_lin_bias_sub_l_kernel(tc, xT, w, b, gate, offs, out):
     with ExitStack() as ctx:
         keep = ctx.enter_context(tc.tile_pool(name="keep", bufs=1))
         psum = ctx.enter_context(tc.psum_pool(name="psum", bufs=1))
-        ring = ctx.enter_context(tc.psum_pool(name="ring", bufs=3))
+        ring = ctx.enter_context(tc.psum_pool(name="ring", bufs=SUM_BANKS))
 
         x_rows = xT.rearrange("(c p t) n -> c t p n", p=P, t=PACK)
         w_rows = w.rearrange("(c p j) m -> c p j m", p=P, j=PACK)
         offsets = keep.tile([P, D * COLS], U16, name="offsets")
+
         columns = keep.tile([P, DEAL], F32, name="columns")
         gate_flat = gate.rearrange("d p v -> (d p v)")
         first = (P - 1) * V
         nc.scalar.dma_start(columns[0 : 2 * QUAD, :], gate_flat[first : first + 2 * V].rearrange("(p i) -> p i", i=DEAL))
         nc.scalar.dma_start(columns[2 * QUAD : 3 * QUAD, :], gate[2, 0, :].rearrange("(p i) -> p i", i=DEAL))
         nc.vector.memset(columns[3 * QUAD : P, :], 0.0)
+
         planes, w_raw = {}, {}
         shared = keep.tile([P, V + PACK * HALF], F32, name="shared")
 
@@ -62,39 +66,41 @@ def tile_picked_bag_lin_bias_sub_l_kernel(tc, xT, w, b, gate, offs, out):
                 nc.sync.dma_start(planes[c, t][:], x_rows[c, t])
                 if (c, t) == (0, 0):
                     nc.sync.dma_start(offsets[:], offs)
-        load_w(0, 0)
-        load_w(0, 1)
-        load_w(1, 0)
-        load_w(1, 1)
+        for c in range(PASSES):
+            for h in range(N // HALF):
+                load_w(c, h)
 
         ident = keep.tile([P, P], F32, name="ident")
         make_identity(nc, ident[:])
         ident_bf = keep.tile([P, P], BF16, name="ident_bf")
         nc.scalar.activation(ident_bf[:], ident[:], IDENT)
+
         gates = keep.tile([P, D, V], F32, name="gates")
         dealt = gates[:].rearrange("q d v -> q (d v)").rearrange("q (p i) -> q p i", i=DEAL)
-        for i0, copy in ((0, nc.vector.tensor_copy), (PACK, nc.scalar.copy)):
-            spread = ring.tile([P, PACK, P], F32, name="sums")
-            for i in range(PACK):
+        for i0, copy in ((0, nc.vector.tensor_copy), (RUN, nc.scalar.copy)):
+            spread = ring.tile([P, RUN, P], F32, name="sums")
+            for i in range(RUN):
                 nc.tensor.transpose(spread[:, i, :], columns[:, i0 + i : i0 + i + 1].to_broadcast([P, P]), ident[:])
-            copy(dealt[:, :, i0 : i0 + PACK], spread[:, :, 0 : 3 * QUAD].rearrange("q i p -> q p i"))
+            copy(dealt[:, :, i0 : i0 + RUN], spread[:, :, 0 : 3 * QUAD].rearrange("q i p -> q p i"))
 
         bias_rows = keep.tile([P, P], F32, name="bias_rows")
         nc.gpsimd.memset(bias_rows[:], 0.0)
         nc.scalar.dma_start(bias_rows[0:M_TILES, :], b.rearrange("(t p) o -> t (p o)", p=P))
-        bias = keep.tile([P, 8], F32, name="bias")
+        bias = keep.tile([P, M_TILES], F32, name="bias")
 
         w_codes = [keep.tile([P, N], U32, name=f"wc{c}", align_bytes=64) for c in range(PASSES)]
         w_scales = [keep.tile([P, N], U8, name=f"ws{c}", align_bytes=64) for c in range(PASSES)]
         w_grouped = [keep.tile([P, N, PACK], BF16, name=f"wg{c}", align_bytes=64) for c in range(PASSES)]
 
-        def round_w(c, m0, m1, copy):
+        def round_w(c, mt0, mt1, copy):
+            m0, m1 = mt0 * P, mt1 * P
             copy(
                 w_grouped[c][:, m0:m1, :].rearrange("p (a i) j -> p a j i", i=RUN),
                 w_raw[c, m0 // HALF][:, :, m0 % HALF : m0 % HALF + m1 - m0].rearrange("p j (a i) -> p a j i", i=RUN),
             )
 
-        def quantize_w(c, m0, m1):
+        def quantize_w(c, mt0, mt1):
+            m0, m1 = mt0 * P, mt1 * P
             nc.vector.quantize_mx(
                 out=w_codes[c][:, m0:m1].bitcast(FP8X4),
                 scales=w_scales[c][:, m0:m1],
@@ -148,64 +154,69 @@ def tile_picked_bag_lin_bias_sub_l_kernel(tc, xT, w, b, gate, offs, out):
                 stop=(c == PASSES - 1),
             )
 
-        def finish(mt, on_scalar):
+        def finish(mt, on_scalar, queue):
             result = keep.tile([P, V], F32, name=f"res{mt}")
             if on_scalar:
                 nc.scalar.activation(result[:], accs[mt][:], IDENT, bias=bias[:, mt : mt + 1])
             else:
                 nc.vector.tensor_scalar(result[:], accs[mt][:], bias[:, mt : mt + 1], None, ADD)
-            queue = nc.scalar if mt == M_TILES - 1 else nc.sync
             queue.dma_start(out[mt * P : (mt + 1) * P, :], result[:])
-
-        S, VV = nc.scalar.copy, nc.vector.tensor_copy
 
         back = psum.tile([P, PACK, V], BF16, name="back")
         for t in range(PACK):
             sum_on_tensor(0, t, back)
         nc.scalar.copy(x_grouped[0][:], back[:].rearrange("p t v -> p v t"))
-        bias_ps = ring.tile([P, P], F32, name="sums")
-        nc.tensor.transpose(bias_ps[:], bias_rows[:], ident[:])
-        nc.scalar.copy(bias[:], bias_ps[:, 0:8])
+        bias_turned = ring.tile([P, P], F32, name="sums")
+        nc.tensor.transpose(bias_turned[:], bias_rows[:], ident[:])
+        nc.scalar.copy(bias[:], bias_turned[:, 0:M_TILES])
 
-        back = psum.tile([P, PACK, V], BF16, name="back")
-        flat = shared[:, 0 : PACK * V // 2].bitcast(BF16).rearrange("p (t v) -> p t v", t=PACK)
-        for t in range(PACK - 1):
+        back = psum.tile([P, PAIR, V], BF16, name="back")
+        pairs = shared[:, 0 : 2 * V].rearrange("p (h v) -> p h v", h=2)
+        for t in range(PAIR):
             sum_on_tensor(1, t, back)
-            if t == PACK - 2:
-                round_w(0, 0, 256, S)
-            nc.scalar.copy(flat[:, t, :], back[:, t, :])
-            if t == 1:
-                quantize_x(0)
-        picked = keep.tile([P, D, V], F32, name="picked_last")
-        partial = keep.tile([P, V], F32, name="partial")
-        gather(picked, 1, PACK - 1, 0, 2)
-        gather(picked, 1, PACK - 1, 2, 3)
-        nc.vector.tensor_tensor(partial[:], picked[:, 0, :], picked[:, 1, :], ADD)
-        round_w(0, 384, 512, VV)
-        nc.vector.tensor_tensor(flat[:, PACK - 1, :], partial[:], picked[:, 2, :], ADD)
+        nc.scalar.copy(
+            pairs[:, 0, :].bitcast(BF16).rearrange("p (v e) -> p v e", e=PAIR), back[:].rearrange("p e v -> p v e")
+        )
+        quantize_x(0)
+        picked = keep.tile([P, PAIR, D, V], F32, name="picked_last")
+        partial = keep.tile([P, PAIR, V], F32, name="partial")
+        for e in range(PAIR):
+            gather(picked[:, e], 1, PAIR + e, 0, D - 1)
+            gather(picked[:, e], 1, PAIR + e, D - 1, D)
+            nc.vector.tensor_tensor(partial[:, e, :], picked[:, e, 0, :], picked[:, e, 1, :], ADD)
 
-        def interleave_x():
-            nc.vector.tensor_copy(
-                x_grouped[1][:].rearrange("p (a i) t -> p a t i", i=RUN),
-                flat.rearrange("p t (a i) -> p a t i", i=RUN),
-            )
+        round_w(0, 0, 2, nc.scalar.copy)
+        round_w(0, 2, 4, nc.scalar.copy)
+        for mt in range(M_TILES - 1):
+            round_w(1, mt, mt + 1, nc.scalar.copy)
 
-        round_w(0, 256, 384, S)
-        round_w(1, 0, 256, S)
-        round_w(1, 256, 384, S)
-        quantize_w(0, 0, 256)
-        interleave_x()
-        quantize_w(0, 256, 512)
+        quantize_w(0, 0, 1)
+        nc.vector.tensor_tensor(
+            pairs[:, 1, :].bitcast(BF16).rearrange("p (v e) -> p v e", e=PAIR),
+            partial[:].rearrange("p e v -> p v e"),
+            picked[:, :, D - 1, :].rearrange("p e v -> p v e"),
+            ADD,
+        )
+        quantize_w(0, 1, 2)
+        nc.vector.tensor_copy(
+            x_grouped[1][:].rearrange("p v t -> p (v t)").bitcast(I32).rearrange("p (v h) -> p v h", h=2),
+            pairs.bitcast(I32).rearrange("p h v -> p v h"),
+        )
+        quantize_w(0, 2, 4)
         quantize_x(1)
         for mt in range(M_TILES):
             product(0, mt)
-        quantize_w(1, 0, 256)
+
+        quantize_w(1, 0, 1)
         product(1, 0)
+        round_w(1, 3, 4, nc.vector.tensor_copy)
+        quantize_w(1, 1, 2)
         product(1, 1)
-        round_w(1, 384, 512, VV)
-        quantize_w(1, 256, 384)
-        quantize_w(1, 384, 512)
-        product(1, 2)
+        quantize_w(1, 3, 4)
+        quantize_w(1, 2, 3)
         product(1, 3)
-        for mt, on_scalar in enumerate((True, True, False, True)):
-            finish(mt, on_scalar)
+        product(1, 2)
+        finish(0, True, nc.sync)
+        finish(1, True, nc.sync)
+        finish(3, False, nc.sync)
+        finish(2, True, nc.scalar)

@@ -62,7 +62,7 @@ def tile_picked_bag_lin_bias_sub_l_kernel(tc, xT, w, b, gate, offs, out):
 
         for c in range(PASSES):
             for t in range(PACK):
-                planes[c, t] = keep.tile([P, T], F32, name=f"plane{c}{t}", tag=f"plane{c}{t}", align_bytes=64)
+                planes[c, t] = keep.tile([P, T], F32, name=f"plane{c}{t}")
                 nc.sync.dma_start(planes[c, t][:], x_rows[c, t])
                 if (c, t) == (0, 0):
                     nc.sync.dma_start(offsets[:], offs)
@@ -73,14 +73,18 @@ def tile_picked_bag_lin_bias_sub_l_kernel(tc, xT, w, b, gate, offs, out):
         ident = keep.tile([P, P], F32, name="ident")
         make_identity(nc, ident[:])
         ident_bf = keep.tile([P, P], BF16, name="ident_bf")
-        nc.scalar.activation(ident_bf[:], ident[:], IDENT)
+        nc.vector.tensor_copy(ident_bf[:], ident[:])
+        columns_bf = keep.tile([P, DEAL], BF16, name="columns_bf")
+        nc.vector.tensor_copy(columns_bf[:], columns[:])
 
         gates = keep.tile([P, D, V], F32, name="gates")
         dealt = gates[:].rearrange("q d v -> q (d v)").rearrange("q (p i) -> q p i", i=DEAL)
         for i0, copy in ((0, nc.vector.tensor_copy), (RUN, nc.scalar.copy)):
-            spread = ring.tile([P, RUN, P], F32, name="sums")
+            spread = ring.tile([P, RUN, P], BF16, name="sums")
             for i in range(RUN):
-                nc.tensor.transpose(spread[:, i, :], columns[:, i0 + i : i0 + i + 1].to_broadcast([P, P]), ident[:])
+                nc.tensor.transpose(
+                    spread[:, i, :], columns_bf[:, i0 + i : i0 + i + 1].to_broadcast([P, P]), ident_bf[:]
+                )
             copy(dealt[:, :, i0 : i0 + RUN], spread[:, :, 0 : 3 * QUAD].rearrange("q i p -> q p i"))
 
         bias_rows = keep.tile([P, P], F32, name="bias_rows")
@@ -116,7 +120,7 @@ def tile_picked_bag_lin_bias_sub_l_kernel(tc, xT, w, b, gate, offs, out):
             )
 
         def sum_on_tensor(c, t, back):
-            picked = keep.tile([P, D, V], F32, name=f"picked{c}{t}")
+            picked = keep.tile([P, D, V], F32, name=f"picked{c}{t}", tag=f"picked{c}{t}", align_bytes=64)
             gather(picked, c, t, 0, D)
             sums = ring.tile([P, U, P], F32, name="sums")
             for u in range(U):
@@ -133,7 +137,7 @@ def tile_picked_bag_lin_bias_sub_l_kernel(tc, xT, w, b, gate, offs, out):
         x_grouped = [keep.tile([P, V, PACK], BF16, name=f"xg{c}", align_bytes=64) for c in range(PASSES)]
 
         def quantize_x(c):
-            x_codes[c] = keep.tile([P, V], U32, name=f"xc{c}", tag=("plane11" if c == 0 else "xc1"), align_bytes=64)
+            x_codes[c] = keep.tile([P, V], U32, name=f"xc{c}", tag=("picked10" if c == 0 else "xc1"), align_bytes=64)
             nc.vector.quantize_mx(
                 out=x_codes[c][:].bitcast(FP8X4),
                 scales=x_scales[c][:],

@@ -169,7 +169,9 @@ def tile_picked_bag_lin_bias_sub_l_kernel(tc, xT, w, b, gate, offs, out):
         back = psum.tile([P, PACK, V], BF16, name="back")
         for t in range(PACK):
             sum_on_tensor(0, t, back)
-        nc.scalar.copy(x_grouped[0][:], back[:].rearrange("p t v -> p v t"))
+        nc.scalar.copy(
+            x_grouped[0][:].rearrange("p (a i) t -> p a t i", i=RUN), back[:].rearrange("p t (a i) -> p a t i", i=RUN)
+        )
         bias_turned = ring.tile([P, P], F32, name="sums")
         nc.tensor.transpose(bias_turned[:], bias_rows[:], ident[:])
         nc.scalar.copy(bias[:], bias_turned[:, 0:M_TILES])
@@ -179,7 +181,8 @@ def tile_picked_bag_lin_bias_sub_l_kernel(tc, xT, w, b, gate, offs, out):
         for t in range(PAIR):
             sum_on_tensor(1, t, back)
         nc.scalar.copy(
-            pairs[:, 0, :].bitcast(BF16).rearrange("p (v e) -> p v e", e=PAIR), back[:].rearrange("p e v -> p v e")
+            pairs[:, 0, :].bitcast(BF16).rearrange("p (a i e) -> p a e i", i=RUN, e=PAIR),
+            back[:].rearrange("p e (a i) -> p a e i", i=RUN),
         )
         quantize_x(0)
         picked = keep.tile([P, PAIR, D, V], F32, name="picked_last")
@@ -196,15 +199,15 @@ def tile_picked_bag_lin_bias_sub_l_kernel(tc, xT, w, b, gate, offs, out):
 
         quantize_w(0, 0, 1)
         nc.vector.tensor_tensor(
-            pairs[:, 1, :].bitcast(BF16).rearrange("p (v e) -> p v e", e=PAIR),
-            partial[:].rearrange("p e v -> p v e"),
-            picked[:, :, D - 1, :].rearrange("p e v -> p v e"),
+            pairs[:, 1, :].bitcast(BF16).rearrange("p (a i e) -> p a e i", i=RUN, e=PAIR),
+            partial[:].rearrange("p e (a i) -> p a e i", i=RUN),
+            picked[:, :, D - 1, :].rearrange("p e (a i) -> p a e i", i=RUN),
             ADD,
         )
         quantize_w(0, 1, 2)
         nc.vector.tensor_copy(
-            x_grouped[1][:].rearrange("p v t -> p (v t)").bitcast(I32).rearrange("p (v h) -> p v h", h=2),
-            pairs.bitcast(I32).rearrange("p h v -> p v h"),
+            x_grouped[1][:].rearrange("p v t -> p (v t)").bitcast(I32).rearrange("p (a i h) -> p a h i", i=RUN, h=2),
+            pairs.bitcast(I32).rearrange("p h (a i) -> p a h i", i=RUN),
         )
         quantize_w(0, 2, 4)
         quantize_x(1)

@@ -70,22 +70,21 @@ def tile_picked_bag_lin_bias_sub_l_kernel(tc, xT, w, b, gate, offs, out):
             for h in range(N // HALF):
                 load_w(c, h)
 
+        ident_bf = keep.tile([P, P], BF16, name="ident_bf")
+        make_identity(nc, ident_bf[:])
         ident = keep.tile([P, P], F32, name="ident")
         make_identity(nc, ident[:])
-        ident_bf = keep.tile([P, P], BF16, name="ident_bf")
-        nc.vector.tensor_copy(ident_bf[:], ident[:])
-        columns_bf = keep.tile([P, DEAL], BF16, name="columns_bf")
-        nc.vector.tensor_copy(columns_bf[:], columns[:])
+        halves = columns[:].bitcast(BF16)
 
         gates = keep.tile([P, D, V], F32, name="gates")
         dealt = gates[:].rearrange("q d v -> q (d v)").rearrange("q (p i) -> q p i", i=DEAL)
-        for i0, copy in ((0, nc.vector.tensor_copy), (RUN, nc.scalar.copy)):
+        for i0 in (0, RUN):
             spread = ring.tile([P, RUN, P], BF16, name="sums")
             for i in range(RUN):
                 nc.tensor.transpose(
-                    spread[:, i, :], columns_bf[:, i0 + i : i0 + i + 1].to_broadcast([P, P]), ident_bf[:]
+                    spread[:, i, :], halves[:, 2 * (i0 + i) + 1 : 2 * (i0 + i) + 2].to_broadcast([P, P]), ident_bf[:]
                 )
-            copy(dealt[:, :, i0 : i0 + RUN], spread[:, :, 0 : 3 * QUAD].rearrange("q i p -> q p i"))
+            nc.scalar.copy(dealt[:, :, i0 : i0 + RUN], spread[:, :, 0 : 3 * QUAD].rearrange("q i p -> q p i"))
 
         bias_rows = keep.tile([P, P], F32, name="bias_rows")
         nc.gpsimd.memset(bias_rows[:], 0.0)
@@ -121,7 +120,14 @@ def tile_picked_bag_lin_bias_sub_l_kernel(tc, xT, w, b, gate, offs, out):
 
         def sum_on_tensor(c, t, back):
             picked = keep.tile([P, D, V], F32, name=f"picked{c}{t}", tag=f"picked{c}{t}", align_bytes=64)
-            gather(picked, c, t, 0, D)
+            if (c, t) == (0, 0):
+                bare = keep.tile([P, D * V], F32, name="bare")
+                nc.vector.tensor_copy(bare[:], planes[c, t][:].indirect(offsets[:]))
+                nc.vector.tensor_tensor(
+                    picked[:].rearrange("p d v -> p (d v)"), bare[:], gates[:].rearrange("p d v -> p (d v)"), MULT
+                )
+            else:
+                gather(picked, c, t, 0, D)
             sums = ring.tile([P, U, P], F32, name="sums")
             for u in range(U):
                 for d in range(D):

@@ -50,14 +50,14 @@ def tile_picked_bag_lin_bias_sub_l_kernel(tc, xT, w, b, gate, offs, out):
         nc.vector.memset(columns[3 * QUAD : P, :], 0.0)
 
         planes, w_raw = {}, {}
-        shared = keep.tile([P, V + PACK * HALF], F32, name="shared")
+        shared_tile = keep.tile([P, (2 + PACK) * HALF], F32, name="shared")
+        shared = shared_tile[:].rearrange("p (r m) -> p r m", m=HALF)
 
         def load_w(c, h):
             if (c, h) == (0, 0):
-                w_raw[c, h] = shared[:, V : V + PACK * HALF].rearrange("p (j m) -> p j m", j=PACK)
+                w_raw[c, h] = shared[:, 2 : 2 + PACK, :]
             else:
-                raw = keep.tile([P, PACK, HALF], F32, name=f"wraw{c}{h}")
-                w_raw[c, h] = raw[:]
+                w_raw[c, h] = keep.tile([P, PACK, HALF], F32, name=f"wraw{c}{h}")[:]
             nc.sync.dma_start(w_raw[c, h], w_rows[c, :, :, h * HALF : (h + 1) * HALF])
 
         for c in range(PASSES):
@@ -183,12 +183,12 @@ def tile_picked_bag_lin_bias_sub_l_kernel(tc, xT, w, b, gate, offs, out):
         nc.scalar.copy(bias[:], bias_turned[:, 0:M_TILES])
 
         back = psum.tile([P, PAIR, V], BF16, name="back")
-        pairs = shared[:, 0 : 2 * V].rearrange("p (h v) -> p h v", h=2)
+        pairs = shared[:, 0 : 2 * U, 0:P].rearrange("p (h u) v -> p h u v", h=2)
         for t in range(PAIR):
             sum_on_tensor(1, t, back)
         nc.scalar.copy(
-            pairs[:, 0, :].bitcast(BF16).rearrange("p (a i e) -> p a e i", i=RUN, e=PAIR),
-            back[:].rearrange("p e (a i) -> p a e i", i=RUN),
+            pairs[:, 0].bitcast(BF16).rearrange("p u (a i e) -> p u a e i", i=RUN, e=PAIR),
+            back[:].rearrange("p e (u a i) -> p u a e i", u=U, i=RUN),
         )
         quantize_x(0)
         picked = keep.tile([P, PAIR, D, V], F32, name="picked_last")
@@ -198,22 +198,24 @@ def tile_picked_bag_lin_bias_sub_l_kernel(tc, xT, w, b, gate, offs, out):
             gather(picked[:, e], 1, PAIR + e, D - 1, D)
             nc.vector.tensor_tensor(partial[:, e, :], picked[:, e, 0, :], picked[:, e, 1, :], ADD)
 
-        round_w(0, 0, 2, nc.scalar.copy)
-        round_w(0, 2, 4, nc.scalar.copy)
-        for mt in range(M_TILES - 1):
-            round_w(1, mt, mt + 1, nc.scalar.copy)
+        for c in range(PASSES):
+            for mt in range(M_TILES - 1):
+                round_w(c, mt, mt + 1, nc.scalar.copy)
 
         quantize_w(0, 0, 1)
-        nc.vector.tensor_tensor(
-            pairs[:, 1, :].bitcast(BF16).rearrange("p (a i e) -> p a e i", i=RUN, e=PAIR),
-            partial[:].rearrange("p e (a i) -> p a e i", i=RUN),
-            picked[:, :, D - 1, :].rearrange("p e (a i) -> p a e i", i=RUN),
-            ADD,
-        )
+        for u in range(U):
+            bags = slice(u * P, (u + 1) * P)
+            nc.vector.tensor_tensor(
+                pairs[:, 1, u, :].bitcast(BF16).rearrange("p (a i e) -> p a e i", i=RUN, e=PAIR),
+                partial[:, :, bags].rearrange("p e (a i) -> p a e i", i=RUN),
+                picked[:, :, D - 1, bags].rearrange("p e (a i) -> p a e i", i=RUN),
+                ADD,
+            )
+        round_w(0, 3, 4, nc.vector.tensor_copy)
         quantize_w(0, 1, 2)
         nc.vector.tensor_copy(
-            x_grouped[1][:].rearrange("p v t -> p (v t)").bitcast(I32).rearrange("p (a i h) -> p a h i", i=RUN, h=2),
-            pairs.bitcast(I32).rearrange("p h (a i) -> p a h i", i=RUN),
+            x_grouped[1][:].rearrange("p v t -> p (v t)").bitcast(I32).rearrange("p (u a i h) -> p u a h i", u=U, i=RUN, h=2),
+            pairs.bitcast(I32).rearrange("p h u (a i) -> p u a h i", i=RUN),
         )
         quantize_w(0, 2, 4)
         quantize_x(1)

@@ -28,6 +28,7 @@ DEAL = 8
 COLS = V // 16
 U = V // P
 M_TILES = N // P
+PAGE = 4096
 SUM_BANKS = 3
 
 
@@ -50,19 +51,19 @@ def tile_picked_bag_lin_bias_sub_l_kernel(tc, xT, w, b, gate, offs, out):
         nc.vector.memset(columns[3 * QUAD : P, :], 0.0)
 
         planes, w_raw = {}, {}
-        shared_tile = keep.tile([P, (2 + PACK) * HALF], F32, name="shared")
+        shared_tile = keep.tile([P, (2 + PACK) * HALF], F32, name="shared", align_bytes=PAGE // 2)
         shared = shared_tile[:].rearrange("p (r m) -> p r m", m=HALF)
 
         def load_w(c, h):
             if (c, h) == (0, 0):
                 w_raw[c, h] = shared[:, 2 : 2 + PACK, :]
             else:
-                w_raw[c, h] = keep.tile([P, PACK, HALF], F32, name=f"wraw{c}{h}")[:]
+                w_raw[c, h] = keep.tile([P, PACK, HALF], F32, name=f"wraw{c}{h}", align_bytes=PAGE)[:]
             nc.sync.dma_start(w_raw[c, h], w_rows[c, :, :, h * HALF : (h + 1) * HALF])
 
         for c in range(PASSES):
             for t in range(PACK):
-                planes[c, t] = keep.tile([P, T], F32, name=f"plane{c}{t}")
+                planes[c, t] = keep.tile([P, T], F32, name=f"plane{c}{t}", align_bytes=PAGE)
                 nc.sync.dma_start(planes[c, t][:], x_rows[c, t])
                 if (c, t) == (0, 0):
                     nc.sync.dma_start(offsets[:], offs)

@@ -16,6 +16,7 @@ FP8X4 = mybir.dt.float8_e4m3fn_x4
 MULT = mybir.AluOpType.mult
 ADD = mybir.AluOpType.add
 IDENT = mybir.ActivationFunctionType.Identity
+COPY = mybir.ActivationFunctionType.Copy
 
 P = 128
 PACK = 4
@@ -195,8 +196,14 @@ def tile_picked_bag_lin_bias_sub_l_kernel(tc, xT, w, b, gate, offs, out):
         picked = keep.tile([P, PAIR, D, V], F32, name="picked_last")
         partial = keep.tile([P, PAIR, V], F32, name="partial")
         for e in range(PAIR):
-            gather(picked[:, e], 1, PAIR + e, 0, D - 1)
-            gather(picked[:, e], 1, PAIR + e, D - 1, D)
+            if e == 0:
+                gather(picked[:, e], 1, PAIR + e, 0, D - 1)
+                gather(picked[:, e], 1, PAIR + e, D - 1, D)
+            else:
+                third = keep.tile([P, V], F32, name="third")
+                nc.scalar.activation(third[:], planes[1, PAIR + e][:].indirect(offsets[:, (D - 1) * COLS : D * COLS]), COPY)
+                gather(picked[:, e], 1, PAIR + e, 0, D - 1)
+                nc.vector.tensor_tensor(picked[:, e, D - 1, :], third[:], gates[:, D - 1, :], MULT)
             nc.vector.tensor_tensor(partial[:, e, :], picked[:, e, 0, :], picked[:, e, 1, :], ADD)
 
         for c in range(PASSES):

@@ -242,4 +242,4 @@ def tile_picked_bag_lin_bias_sub_l_kernel(tc, xT, w, b, gate, offs, out):
         finish(0, True, nc.sync)
         finish(1, True, nc.sync)
         finish(3, False, nc.sync)
-        finish(2, True, nc.scalar)
+        finish(2, True, nc.sync)

from contextlib import ExitStack

import concourse.mybir as mybir
from concourse.masks import make_identity

K, T, D, V, N = 1024, 2048, 3, 256, 512
FLOPS = 2 * K * N * V

F32 = mybir.dt.float32
BF16 = mybir.dt.bfloat16
U32 = mybir.dt.uint32
I32 = mybir.dt.int32
U16 = mybir.dt.uint16
U8 = mybir.dt.uint8
FP8X4 = mybir.dt.float8_e4m3fn_x4
MULT = mybir.AluOpType.mult
ADD = mybir.AluOpType.add
IDENT = mybir.ActivationFunctionType.Identity
COPY = mybir.ActivationFunctionType.Copy

P = 128
PACK = 4
PAIR = 2
PASSES = K // (P * PACK)
HALF = N // 2
RUN = 4
QUAD = 32
DEAL = 8
COLS = V // 16
U = V // P
M_TILES = N // P
PAGE = 4096
SUM_BANKS = 3


def tile_picked_bag_lin_bias_sub_l_kernel(tc, xT, w, b, gate, offs, out):
    nc = tc.nc
    with ExitStack() as ctx:
        keep = ctx.enter_context(tc.tile_pool(name="keep", bufs=1))
        psum = ctx.enter_context(tc.psum_pool(name="psum", bufs=1))
        ring = ctx.enter_context(tc.psum_pool(name="ring", bufs=SUM_BANKS))

        x_rows = xT.rearrange("(c p t) n -> c t p n", p=P, t=PACK)
        w_rows = w.rearrange("(c p j) m -> c p j m", p=P, j=PACK)
        offsets = keep.tile([P, D * COLS], U16, name="offsets")

        columns = keep.tile([P, DEAL], F32, name="columns")
        gate_flat = gate.rearrange("d p v -> (d p v)")
        first = (P - 1) * V
        nc.scalar.dma_start(columns[0 : 2 * QUAD, :], gate_flat[first : first + 2 * V].rearrange("(p i) -> p i", i=DEAL))
        nc.scalar.dma_start(columns[2 * QUAD : 3 * QUAD, :], gate[2, 0, :].rearrange("(p i) -> p i", i=DEAL))
        nc.vector.memset(columns[3 * QUAD : P, :], 0.0)

        planes, w_raw = {}, {}
        shared_tile = keep.tile([P, (2 + PACK) * HALF], F32, name="shared", align_bytes=PAGE // 2)
        shared = shared_tile[:].rearrange("p (r m) -> p r m", m=HALF)

        def load_w(c, h):
            if (c, h) == (0, 0):
                w_raw[c, h] = shared[:, 2 : 2 + PACK, :]
            else:
                w_raw[c, h] = keep.tile([P, PACK, HALF], F32, name=f"wraw{c}{h}", align_bytes=PAGE)[:]
            nc.sync.dma_start(w_raw[c, h], w_rows[c, :, :, h * HALF : (h + 1) * HALF])

        for c in range(PASSES):
            for t in range(PACK):
                planes[c, t] = keep.tile([P, T], F32, name=f"plane{c}{t}", align_bytes=PAGE)
                nc.sync.dma_start(planes[c, t][:], x_rows[c, t])
                if (c, t) == (0, 0):
                    nc.sync.dma_start(offsets[:], offs)
        for c in range(PASSES):
            for h in range(N // HALF):
                load_w(c, h)

        ident_bf = keep.tile([P, P], BF16, name="ident_bf")
        make_identity(nc, ident_bf[:])
        ident = keep.tile([P, P], F32, name="ident")
        make_identity(nc, ident[:])
        halves = columns[:].bitcast(BF16)

        gates = keep.tile([P, D, V], F32, name="gates")
        dealt = gates[:].rearrange("q d v -> q (d v)").rearrange("q (p i) -> q p i", i=DEAL)
        for i0 in (0, RUN):
            spread = ring.tile([P, RUN, P], BF16, name="sums")
            for i in range(RUN):
                nc.tensor.transpose(
                    spread[:, i, :], halves[:, 2 * (i0 + i) + 1 : 2 * (i0 + i) + 2].to_broadcast([P, P]), ident_bf[:]
                )
            nc.scalar.copy(dealt[:, :, i0 : i0 + RUN], spread[:, :, 0 : 3 * QUAD].rearrange("q i p -> q p i"))

        bias_rows = keep.tile([P, P], F32, name="bias_rows")
        nc.gpsimd.memset(bias_rows[:], 0.0)
        nc.scalar.dma_start(bias_rows[0:M_TILES, :], b.rearrange("(t p) o -> t (p o)", p=P))
        bias = keep.tile([P, M_TILES], F32, name="bias")

        w_codes = [keep.tile([P, N], U32, name=f"wc{c}", align_bytes=64) for c in range(PASSES)]
        w_scales = [keep.tile([P, N], U8, name=f"ws{c}", align_bytes=64) for c in range(PASSES)]
        w_grouped = [keep.tile([P, N, PACK], BF16, name=f"wg{c}", align_bytes=64) for c in range(PASSES)]

        def round_w(c, mt0, mt1, copy):
            m0, m1 = mt0 * P, mt1 * P
            copy(
                w_grouped[c][:, m0:m1, :].rearrange("p (a i) j -> p a j i", i=RUN),
                w_raw[c, m0 // HALF][:, :, m0 % HALF : m0 % HALF + m1 - m0].rearrange("p j (a i) -> p a j i", i=RUN),
            )

        def quantize_w(c, mt0, mt1):
            m0, m1 = mt0 * P, mt1 * P
            nc.vector.quantize_mx(
                out=w_codes[c][:, m0:m1].bitcast(FP8X4),
                scales=w_scales[c][:, m0:m1],
                in_=w_grouped[c][:, m0:m1, :].rearrange("p m j -> p (m j)"),
            )

        def gather(picked, c, t, d0, d1):
            nc.vector.tensor_tensor(
                picked[:, d0:d1, :].rearrange("p d v -> p (d v)"),
                planes[c, t][:].indirect(offsets[:, d0 * COLS : d1 * COLS]),
                gates[:, d0:d1, :].rearrange("p d v -> p (d v)"),
                MULT,
            )

        def sum_on_tensor(c, t, back):
            picked = keep.tile([P, D, V], F32, name=f"picked{c}{t}", tag=f"picked{c}{t}", align_bytes=64)
            if (c, t) == (0, 0):
                bare = keep.tile([P, D * V], F32, name="bare")
                nc.vector.tensor_copy(bare[:], planes[c, t][:].indirect(offsets[:]))
                nc.vector.tensor_tensor(
                    picked[:].rearrange("p d v -> p (d v)"), bare[:], gates[:].rearrange("p d v -> p (d v)"), MULT
                )
            else:
                gather(picked, c, t, 0, D)
            sums = ring.tile([P, U, P], F32, name="sums")
            for u in range(U):
                for d in range(D):
                    nc.tensor.matmul(sums[:, u, :], lhsT=picked[:, d, u * P : (u + 1) * P], rhs=ident[:],
                                     start=(d == 0), stop=(d == D - 1), is_transpose=True)
            turned = keep.tile([P, U, P], BF16, name=f"turned{c}{t}")
            nc.scalar.copy(turned[:], sums[:])
            for u in range(U):
                nc.tensor.transpose(back[:, t, u * P : (u + 1) * P], turned[:, u, :], ident_bf[:])

        x_codes = {}
        x_scales = [keep.tile([P, V], U8, name=f"xs{c}", align_bytes=64) for c in range(PASSES)]
        x_grouped = [keep.tile([P, V, PACK], BF16, name=f"xg{c}", align_bytes=64) for c in range(PASSES)]

        def quantize_x(c):
            x_codes[c] = keep.tile([P, V], U32, name=f"xc{c}", tag=("picked10" if c == 0 else "xc1"), align_bytes=64)
            nc.vector.quantize_mx(
                out=x_codes[c][:].bitcast(FP8X4),
                scales=x_scales[c][:],
                in_=x_grouped[c][:].rearrange("p v t -> p (v t)"),
            )

        accs = [psum.tile([P, V], F32, name=f"acc{mt}") for mt in range(M_TILES)]

        def product(c, mt):
            cols = slice(mt * P, (mt + 1) * P)
            nc.tensor.matmul_mx(
                out=accs[mt][:],
                lhsT=w_codes[c][:, cols].bitcast(FP8X4),
                lhsT_scale=w_scales[c][:, cols],
                rhs=x_codes[c][:].bitcast(FP8X4),
                rhs_scale=x_scales[c][:],
                start=(c == 0),
                stop=(c == PASSES - 1),
            )

        def finish(mt, on_scalar, queue):
            result = keep.tile([P, V], F32, name=f"res{mt}")
            if on_scalar:
                nc.scalar.activation(result[:], accs[mt][:], IDENT, bias=bias[:, mt : mt + 1])
            else:
                nc.vector.tensor_scalar(result[:], accs[mt][:], bias[:, mt : mt + 1], None, ADD)
            queue.dma_start(out[mt * P : (mt + 1) * P, :], result[:])

        back = psum.tile([P, PACK, V], BF16, name="back")
        for t in range(PACK):
            sum_on_tensor(0, t, back)
        nc.scalar.copy(
            x_grouped[0][:].rearrange("p (a i) t -> p a t i", i=RUN), back[:].rearrange("p t (a i) -> p a t i", i=RUN)
        )
        bias_turned = ring.tile([P, P], F32, name="sums")
        nc.tensor.transpose(bias_turned[:], bias_rows[:], ident[:])
        nc.scalar.copy(bias[:], bias_turned[:, 0:M_TILES])

        back = psum.tile([P, PAIR, V], BF16, name="back")
        pairs = shared[:, 0 : 2 * U, 0:P].rearrange("p (h u) v -> p h u v", h=2)
        for t in range(PAIR):
            sum_on_tensor(1, t, back)
        nc.scalar.copy(
            pairs[:, 0].bitcast(BF16).rearrange("p u (a i e) -> p u a e i", i=RUN, e=PAIR),
            back[:].rearrange("p e (u a i) -> p u a e i", u=U, i=RUN),
        )
        quantize_x(0)
        picked = keep.tile([P, PAIR, D, V], F32, name="picked_last")
        partial = keep.tile([P, PAIR, V], F32, name="partial")
        for e in range(PAIR):
            if e == 0:
                gather(picked[:, e], 1, PAIR + e, 0, D - 1)
                gather(picked[:, e], 1, PAIR + e, D - 1, D)
            else:
                third = keep.tile([P, V], F32, name="third")
                nc.scalar.activation(third[:], planes[1, PAIR + e][:].indirect(offsets[:, (D - 1) * COLS : D * COLS]), COPY)
                gather(picked[:, e], 1, PAIR + e, 0, D - 1)
                nc.vector.tensor_tensor(picked[:, e, D - 1, :], third[:], gates[:, D - 1, :], MULT)
            nc.vector.tensor_tensor(partial[:, e, :], picked[:, e, 0, :], picked[:, e, 1, :], ADD)

        for c in range(PASSES):
            for mt in range(M_TILES - 1):
                round_w(c, mt, mt + 1, nc.scalar.copy)

        quantize_w(0, 0, 1)
        for u in range(U):
            bags = slice(u * P, (u + 1) * P)
            nc.vector.tensor_tensor(
                pairs[:, 1, u, :].bitcast(BF16).rearrange("p (a i e) -> p a e i", i=RUN, e=PAIR),
                partial[:, :, bags].rearrange("p e (a i) -> p a e i", i=RUN),
                picked[:, :, D - 1, bags].rearrange("p e (a i) -> p a e i", i=RUN),
                ADD,
            )
        round_w(0, 3, 4, nc.vector.tensor_copy)
        quantize_w(0, 1, 2)
        nc.vector.tensor_copy(
            x_grouped[1][:].rearrange("p v t -> p (v t)").bitcast(I32).rearrange("p (u a i h) -> p u a h i", u=U, i=RUN, h=2),
            pairs.bitcast(I32).rearrange("p h u (a i) -> p u a h i", i=RUN),
        )
        quantize_w(0, 2, 4)
        quantize_x(1)
        for mt in range(M_TILES):
            product(0, mt)

        quantize_w(1, 0, 1)
        product(1, 0)
        round_w(1, 3, 4, nc.vector.tensor_copy)
        quantize_w(1, 1, 2)
        product(1, 1)
        quantize_w(1, 3, 4)
        quantize_w(1, 2, 3)
        product(1, 3)
        product(1, 2)
        finish(0, True, nc.sync)
        finish(1, True, nc.sync)
        finish(3, False, nc.sync)
        finish(2, True, nc.sync)
